import numpy as np
import ml_dtypes


def mxq(x, axis, fmt="e4m3"):
    dtype, down = {"e4m3": (ml_dtypes.float8_e4m3fn, 7), "e5m2": (ml_dtypes.float8_e5m2, 14)}[fmt]
    v = np.moveaxis(np.asarray(x, np.float32).astype(ml_dtypes.bfloat16).astype(np.float64), axis, -1)
    blocks = v.reshape(v.shape[:-1] + (-1, 32))
    amax = np.abs(blocks).max(-1, keepdims=True)
    byte = np.maximum(np.where(amax > 0, np.frexp(amax)[1] - 1 + 127, 0) - down, 1)
    scale = np.exp2(byte - 127.0)
    codes = (blocks / scale).astype(np.float32).astype(dtype).astype(np.float64)
    return np.moveaxis((codes * scale).reshape(v.shape), -1, axis)


WIDE = False


def mx_kscale(k):
    if not WIDE:
        return np.ones(k)
    levels = np.array([10, -10, 5, -5, 0])
    if k % 512:
        return np.exp2(np.random.permutation(np.resize(levels, k // 32))).repeat(32)
    a = np.empty((k // 512, 16))
    for p in range(k // 512):
        a[p, :8] = np.random.permutation(np.resize(levels, 8))
        for g in range(8):
            far = levels[np.abs(levels - a[p, g]) >= 10]
            a[p, g + 8] = far[np.random.randint(len(far))]
    return np.exp2(a.ravel()).repeat(32)


def f64(x):
    return np.asarray(x).astype(np.float64)


def striped8(idx):
    return np.concatenate([v.reshape(-1, 16).T for v in idx]).astype(np.uint16)


def unstriped8(offs):
    return np.stack([offs[16 * g:16 * g + 16].T.reshape(-1) for g in range(8)]).astype(np.int64)


E2M1 = np.array([0.0, 0.5, 1.0, 1.5, 2.0, 3.0, 4.0, 6.0, -0.0, -0.5, -1.0, -1.5, -2.0, -3.0, -4.0, -6.0])


def pack_weight(w, fmt):
    k, n = w.shape
    w = f64(np.asarray(w, np.float32).astype(ml_dtypes.bfloat16)).reshape(k // 32, 32, n)
    amax = np.abs(w).max(1)
    if fmt == "e4m3":
        byte = np.frexp(amax)[1] - 1 + 127 - 7
    else:
        mant, ex = np.frexp(amax / 6.0)
        byte = np.where(mant > 0.5, ex, ex - 1) + 127
    byte = np.clip(np.where(amax > 0, byte, 1), 1, 254)
    scaled = (w * np.exp2(127.0 - byte)[:, None, :]).reshape(k, n).astype(np.float32)
    by_word = np.ascontiguousarray(scaled.reshape(k // 512, 128, 4, n).transpose(0, 1, 3, 2))
    if fmt == "e4m3":
        words = by_word.astype(ml_dtypes.float8_e4m3fn).view(np.uint8)
    else:
        c = by_word.astype(ml_dtypes.float4_e2m1fn).view(np.uint8) & 0xF
        words = (c[..., 0::2] | (c[..., 1::2] << 4)).reshape(k // 512, 128, 2 * n)
    return np.ascontiguousarray(words), np.ascontiguousarray(byte.astype(np.uint8).reshape(k // 512, 16, n))


def unpack_weight(words, scales, fmt):
    g, _, n = scales.shape
    words = np.ascontiguousarray(words).reshape(g, 128, n, -1)
    if fmt == "e4m3":
        vals = words.view(ml_dtypes.float8_e4m3fn).astype(np.float64)
    else:
        nib = np.empty((g, 128, n, 4), np.uint8)
        nib[..., 0::2] = words & 0xF
        nib[..., 1::2] = words >> 4
        vals = E2M1[nib]
    vals = vals * np.repeat(np.exp2(scales.astype(np.float64) - 127.0), 8, axis=1)[..., None]
    return vals.transpose(0, 1, 3, 2).reshape(g * 512, n)


def gelu(v):
    return 0.5 * v * (1.0 + np.tanh(np.sqrt(2.0 / np.pi) * (v + 0.044715 * v**3)))


K, M, T, S = 512, 256, 2048, 1024


def setup_inputs():
    n = np.random.standard_normal
    s = mx_kscale(K)[:, None]
    p_w = pack_weight(n((K, M)) / np.sqrt(K) / s, "e4m3")
    return {
        "xT": (n((K, T)) * s).astype(np.float32),
        "w_words": p_w[0],
        "w_scales": p_w[1],
        "wgt": np.repeat(np.random.uniform(0.5, 2.0, (8, S)), 16, axis=0).astype(np.float32),
        "b": (0.3 * n(256)).astype(np.float32),
        "offs": striped8(np.stack([np.random.permutation(T)[:S] for _ in range(8)])),
    }


def reference(xT, w_words, w_scales, wgt, b, offs):
    idx = unstriped8(offs)
    group = np.arange(K) % 512 // 64
    xg = f64(wgt)[np.arange(K) // 4 % 128] * f64(xT)[np.arange(K)[:, None], idx[group]]
    xT_ = mxq(xg, 0, "e4m3")
    w_ = unpack_weight(w_words, w_scales, "e4m3")
    y = w_.T @ xT_
    return gelu(y + f64(b)[:, None])

@@ -1,0 +1,144 @@
+from contextlib import ExitStack
+
+import concourse.mybir as mybir
+
+K, M, T, S = 512, 256, 2048, 1024
+FLOPS = 2 * K * M * S
+
+F32 = mybir.dt.float32
+BF16 = mybir.dt.bfloat16
+I32 = mybir.dt.int32
+U32 = mybir.dt.uint32
+U16 = mybir.dt.uint16
+U8 = mybir.dt.uint8
+FP8X4 = mybir.dt.float8_e4m3fn_x4
+MULT = mybir.AluOpType.mult
+GELU = mybir.ActivationFunctionType.Gelu_apprx_tanh
+COPY = mybir.ActivationFunctionType.Copy
+
+P = 128
+PACK = 4
+LOADS = ((0, 128), (128, 384), (384, 1024))
+CHUNKS = ((0, 256), (256, 512), (512, 768), (768, 1024))
+
+
+def tile_list_heads_gelu_kernel(tc, xT, w_words, w_scales, wgt, b, offs, out):
+    nc = tc.nc
+    planes = xT.rearrange("(p i) t -> i p t", i=PACK)
+    with ExitStack() as ctx:
+        keep = ctx.enter_context(tc.tile_pool(name="keep", bufs=1))
+        psum = ctx.enter_context(tc.psum_pool(name="psum", bufs=1))
+
+        offsets = keep.tile([P, S // 16], U16, name="offsets")
+        table = [keep.tile([P, T], F32, name=f"table{i}") for i in range(PACK)]
+        weights = keep.tile([P, S], F32, name="weights")
+        w_codes = keep.tile([P, M], U32, align_bytes=64, name="w_codes")
+        w_planes = keep.tile([P, M], U8, align_bytes=64, name="w_planes")
+        bias = keep.tile([P, M // P], F32, name="bias")
+        cuts = (0, 1024)
+        picked = [keep.tile([P, PACK, cuts[c + 1] - cuts[c]], F32, name=f"picked{c}") for c in range(len(cuts) - 1)]
+        grouped = keep.tile([P, S, PACK], BF16, align_bytes=64, name="grouped")
+        codes = keep.tile([P, S], U32, align_bytes=64, name="codes")
+        scales = keep.tile([P, S], U8, align_bytes=64, name="scales")
+        warm = keep.tile([P, 2], F32, name="warm")
+        result = keep.tile([P, M // P, S], F32, name="result")
+        banks = [psum.tile([P, 512], F32, name=f"bank{i}") for i in range(8)]
+
+        nc.sync.dma_start(table[0][:], planes[0])
+        nc.sync.dma_start(offsets[:], offs)
+        for lo, hi in LOADS:
+            nc.sync.dma_start(weights[:, lo:hi], wgt[:, lo:hi])
+        for i in range(1, PACK):
+            nc.sync.dma_start(table[i][:], planes[i])
+        nc.vector.memset(w_planes[:].bitcast(U32), 0)
+        nc.vector.memset(warm[:, 0:1], 0.0)
+        nc.scalar.activation(warm[:, 1:2], warm[:, 0:1], GELU)
+
+        nc.sync.dma_start(w_codes[:].bitcast(I32), w_words[0].rearrange("p n i -> p (n i)").bitcast(I32))
+        for q in range(4):
+            nc.sync.dma_start(
+                w_planes[32 * q : 32 * q + 4, :].bitcast(I32),
+                w_scales[0, 4 * q : 4 * q + 4, :].bitcast(I32),
+            )
+        with nc.allow_non_contiguous_dma(reason="256 bias values, one a partition"):
+            nc.sync.dma_start(bias[:], b.rearrange("(m p) -> p m", p=P))
+
+        def spot(lo):
+            return max(c for c in range(len(cuts) - 1) if cuts[c] <= lo)
+
+        def gather(i, lo, hi):
+            c = spot(lo)
+            nc.vector.tensor_tensor(
+                picked[c][:, i, lo - cuts[c] : hi - cuts[c]],
+                table[i][:].indirect(offsets[:, lo // 16 : hi // 16]),
+                weights[:, lo:hi],
+                MULT,
+            )
+
+        def interleave(engine, pair, lo, hi):
+            c = spot(lo)
+            src = picked[c][:, pair, lo - cuts[c] : hi - cuts[c]].rearrange("p t c -> p c t")
+            dst = grouped[:, lo:hi, pair]
+            if engine == "V":
+                nc.vector.tensor_copy(dst, src)
+            else:
+                nc.scalar.activation(dst, src, COPY)
+
+        def quantize(lo, hi):
+            nc.vector.quantize_mx(
+                out=codes[:, lo:hi].bitcast(FP8X4),
+                scales=scales[:, lo:hi],
+                in_=grouped[:, lo:hi, :].rearrange("p c t -> p (c t)"),
+            )
+
+        def multiply(bank, at, lo, hi):
+            for m in range(M // P):
+                nc.tensor.matmul_mx(
+                    out=banks[2 * bank + m][:, at : at + hi - lo],
+                    lhsT=w_codes[:, m * P : (m + 1) * P].bitcast(FP8X4),
+                    lhsT_scale=w_planes[:, m * P : (m + 1) * P],
+                    rhs=codes[:, lo:hi].bitcast(FP8X4),
+                    rhs_scale=scales[:, lo:hi],
+                    start=True,
+                    stop=True,
+                )
+
+        def finish(bank, lo, hi):
+            for m in range(M // P):
+                nc.scalar.activation(result[:, m, lo:hi], banks[2 * bank + m][:, 0 : hi - lo], GELU, bias=bias[:, m : m + 1])
+                nc.sync.dma_start(out[m * P : (m + 1) * P, lo:hi], result[:, m, lo:hi])
+
+        lo_pair, hi_pair = slice(0, 2), slice(2, 4)
+        gather(0, 0, 128)
+        gather(0, 128, 384)
+        gather(0, 384, 1024)
+        gather(1, 0, 256)
+        interleave("S", lo_pair, 0, 256)
+        gather(1, 256, 512)
+        interleave("S", lo_pair, 256, 512)
+        gather(1, 512, 1024)
+        interleave("S", lo_pair, 512, 1024)
+        gather(2, 0, 512)
+        gather(2, 512, 1024)
+        gather(3, 0, 256)
+        interleave("S", hi_pair, 0, 256)
+        gather(3, 256, 512)
+        interleave("S", hi_pair, 256, 512)
+        gather(3, 512, 1024)
+        quantize(0, 256)
+        multiply(0, 0, 0, 256)
+        finish(0, 0, 256)
+        interleave("V", hi_pair, 512, 768)
+        quantize(256, 512)
+        multiply(1, 0, 256, 512)
+        finish(1, 256, 512)
+        interleave("V", hi_pair, 768, 1024)
+        quantize(512, 768)
+        multiply(2, 0, 512, 768)
+        finish(2, 512, 768)
+        quantize(768, 896)
+        quantize(896, 1024)
+        multiply(3, 0, 768, 896)
+        multiply(0, 0, 896, 1024)
+        finish(3, 768, 896)
+        finish(0, 896, 1024)

@@ -1,6 +1,7 @@
 from contextlib import ExitStack
 
 import concourse.mybir as mybir
+from concourse.masks import make_identity
 
 K, M, T, S = 512, 256, 2048, 1024
 FLOPS = 2 * K * M * S
@@ -18,8 +19,9 @@ COPY = mybir.ActivationFunctionType.Copy
 
 P = 128
 PACK = 4
-LOADS = ((0, 128), (128, 384), (384, 1024))
-CHUNKS = ((0, 256), (256, 512), (512, 768), (768, 1024))
+GROUPS = 8
+QUARTER = S // 4
+CHUNKS = ((0, 256), (256, 512), (512, 768), (768, 896), (896, 1024))
 
 
 def tile_list_heads_gelu_kernel(tc, xT, w_words, w_scales, wgt, b, offs, out):
@@ -32,27 +34,51 @@ def tile_list_heads_gelu_kernel(tc, xT, w_words, w_scales, wgt, b, offs, out):
         offsets = keep.tile([P, S // 16], U16, name="offsets")
         table = [keep.tile([P, T], F32, name=f"table{i}") for i in range(PACK)]
         weights = keep.tile([P, S], F32, name="weights")
+        compact = keep.tile([P, QUARTER], F32, name="compact")
+        identity = keep.tile([P, P], F32, name="identity")
+        spread = [[keep.tile([P, 2, GROUPS, 16], F32, name=f"spread{half}{h}") for h in range(2)] for half in range(2)]
         w_codes = keep.tile([P, M], U32, align_bytes=64, name="w_codes")
         w_planes = keep.tile([P, M], U8, align_bytes=64, name="w_planes")
         bias = keep.tile([P, M // P], F32, name="bias")
-        cuts = (0, 1024)
-        picked = [keep.tile([P, PACK, cuts[c + 1] - cuts[c]], F32, name=f"picked{c}") for c in range(len(cuts) - 1)]
-        grouped = keep.tile([P, S, PACK], BF16, align_bytes=64, name="grouped")
+        early = keep.tile([P, 2, S], F32, name="early")
+        late = keep.tile([P, 6, QUARTER], F32, name="late")
+        grouped = [
+            keep.tile([P, hi - lo, PACK], BF16, align_bytes=64, name=f"grouped{c}") for c, (lo, hi) in enumerate(CHUNKS)
+        ]
         codes = keep.tile([P, S], U32, align_bytes=64, name="codes")
         scales = keep.tile([P, S], U8, align_bytes=64, name="scales")
         warm = keep.tile([P, 2], F32, name="warm")
         result = keep.tile([P, M // P, S], F32, name="result")
         banks = [psum.tile([P, 512], F32, name=f"bank{i}") for i in range(8)]
 
+        runs = wgt.rearrange("p (q c) -> (p q) c", c=QUARTER)
+        for half in range(2):
+            nc.sync.dma_start(compact[16 * half : 16 * half + 16, :], runs[256 * half : 256 * half + 256 : 17, :])
         nc.sync.dma_start(table[0][:], planes[0])
         nc.sync.dma_start(offsets[:], offs)
-        for lo, hi in LOADS:
-            nc.sync.dma_start(weights[:, lo:hi], wgt[:, lo:hi])
         for i in range(1, PACK):
             nc.sync.dma_start(table[i][:], planes[i])
-        nc.vector.memset(w_planes[:].bitcast(U32), 0)
+        make_identity(nc, identity[:])
+        nc.vector.memset(compact[32:64, :], 0.0)
+        nc.vector.memset(compact[64:128, :], 0.0)
         nc.vector.memset(warm[:, 0:1], 0.0)
         nc.scalar.activation(warm[:, 1:2], warm[:, 0:1], GELU)
+        nc.vector.memset(w_planes[:].bitcast(U32), 0)
+
+        for h in range(2):
+            nc.tensor.transpose(banks[6 + h][:, 0:P], compact[:, h * P : (h + 1) * P], identity[:])
+        for half in range(2):
+            for h, copy in enumerate((nc.vector.tensor_copy, nc.scalar.copy)):
+                turned = banks[6 + h][:, 0:32].rearrange("p (g q) -> p q g", q=4)[:, 2 * half : 2 * half + 2, :]
+                copy(spread[half][h][:], turned.unsqueeze(3).to_broadcast([P, 2, GROUPS, 16]))
+        for q in range(4):
+            for h in range(2):
+                nc.tensor.transpose(
+                    banks[q][:, h * P : (h + 1) * P],
+                    spread[q // 2][h][:, q % 2].rearrange("p g r -> p (g r)"),
+                    identity[:],
+                )
+            nc.scalar.copy(weights[:, q * QUARTER : (q + 1) * QUARTER], banks[q][:, 0:QUARTER])
 
         nc.sync.dma_start(w_codes[:].bitcast(I32), w_words[0].rearrange("p n i -> p (n i)").bitcast(I32))
         for q in range(4):
@@ -63,38 +89,33 @@ def tile_list_heads_gelu_kernel(tc, xT, w_words, w_scales, wgt, b, offs, out):
         with nc.allow_non_contiguous_dma(reason="256 bias values, one a partition"):
             nc.sync.dma_start(bias[:], b.rearrange("(m p) -> p m", p=P))
 
-        def spot(lo):
-            return max(c for c in range(len(cuts) - 1) if cuts[c] <= lo)
+        def gather(i, dst, lo, hi):
+            nc.vector.tensor_tensor(dst, table[i][:].indirect(offsets[:, lo // 16 : hi // 16]), weights[:, lo:hi], MULT)
 
-        def gather(i, lo, hi):
-            c = spot(lo)
-            nc.vector.tensor_tensor(
-                picked[c][:, i, lo - cuts[c] : hi - cuts[c]],
-                table[i][:].indirect(offsets[:, lo // 16 : hi // 16]),
-                weights[:, lo:hi],
-                MULT,
-            )
-
-        def interleave(engine, pair, lo, hi):
-            c = spot(lo)
-            src = picked[c][:, pair, lo - cuts[c] : hi - cuts[c]].rearrange("p t c -> p c t")
-            dst = grouped[:, lo:hi, pair]
-            if engine == "V":
-                nc.vector.tensor_copy(dst, src)
+        def interleave(engine, pair, c):
+            lo, hi = CHUNKS[c]
+            q = lo // QUARTER
+            if pair:
+                rows = slice(q, q + 4, 3) if q < 3 else slice(0, 2)
+                src = late[:, rows, lo - q * QUARTER : hi - q * QUARTER]
             else:
-                nc.scalar.activation(dst, src, COPY)
+                src = early[:, :, lo:hi]
+            dst = grouped[c][:, :, 2 * pair : 2 * pair + 2]
+            if engine == "V":
+                nc.vector.tensor_copy(dst, src.rearrange("p t c -> p c t"))
+            else:
+                nc.scalar.activation(dst, src.rearrange("p t c -> p c t"), COPY)
 
-        def quantize(lo, hi):
+        def quantize(c):
+            lo, hi = CHUNKS[c]
             nc.vector.quantize_mx(
                 out=codes[:, lo:hi].bitcast(FP8X4),
                 scales=scales[:, lo:hi],
-                in_=grouped[:, lo:hi, :].rearrange("p c t -> p (c t)"),
+                in_=grouped[c][:].rearrange("p c t -> p (c t)"),
             )
-
-        def multiply(bank, at, lo, hi):
             for m in range(M // P):
                 nc.tensor.matmul_mx(
-                    out=banks[2 * bank + m][:, at : at + hi - lo],
+                    out=banks[(2 * c + m) % 8][:, 0 : hi - lo],
                     lhsT=w_codes[:, m * P : (m + 1) * P].bitcast(FP8X4),
                     lhsT_scale=w_planes[:, m * P : (m + 1) * P],
                     rhs=codes[:, lo:hi].bitcast(FP8X4),
@@ -103,42 +124,39 @@ def tile_list_heads_gelu_kernel(tc, xT, w_words, w_scales, wgt, b, offs, out):
                     stop=True,
                 )
 
-        def finish(bank, lo, hi):
+        def finish(c):
+            lo, hi = CHUNKS[c]
             for m in range(M // P):
-                nc.scalar.activation(result[:, m, lo:hi], banks[2 * bank + m][:, 0 : hi - lo], GELU, bias=bias[:, m : m + 1])
+                nc.scalar.activation(
+                    result[:, m, lo:hi], banks[(2 * c + m) % 8][:, 0 : hi - lo], GELU, bias=bias[:, m : m + 1]
+                )
                 nc.sync.dma_start(out[m * P : (m + 1) * P, lo:hi], result[:, m, lo:hi])
 
-        lo_pair, hi_pair = slice(0, 2), slice(2, 4)
-        gather(0, 0, 128)
-        gather(0, 128, 384)
-        gather(0, 384, 1024)
-        gather(1, 0, 256)
-        interleave("S", lo_pair, 0, 256)
-        gather(1, 256, 512)
-        interleave("S", lo_pair, 256, 512)
-        gather(1, 512, 1024)
-        interleave("S", lo_pair, 512, 1024)
-        gather(2, 0, 512)
-        gather(2, 512, 1024)
-        gather(3, 0, 256)
-        interleave("S", hi_pair, 0, 256)
-        gather(3, 256, 512)
-        interleave("S", hi_pair, 256, 512)
-        gather(3, 512, 1024)
-        quantize(0, 256)
-        multiply(0, 0, 0, 256)
-        finish(0, 0, 256)
-        interleave("V", hi_pair, 512, 768)
-        quantize(256, 512)
-        multiply(1, 0, 256, 512)
-        finish(1, 256, 512)
-        interleave("V", hi_pair, 768, 1024)
-        quantize(512, 768)
-        multiply(2, 0, 512, 768)
-        finish(2, 512, 768)
-        quantize(768, 896)
-        quantize(896, 1024)
-        multiply(3, 0, 768, 896)
-        multiply(0, 0, 896, 1024)
-        finish(3, 768, 896)
-        finish(0, 896, 1024)
+        gather(0, early[:, 0, 0:256], 0, 256)
+        gather(0, early[:, 0, 256:512], 256, 512)
+        gather(0, early[:, 0, 512:1024], 512, 1024)
+        gather(1, early[:, 1, 0:512], 0, 512)
+        interleave("S", 0, 0)
+        interleave("S", 0, 1)
+        gather(1, early[:, 1, 512:1024], 512, 1024)
+        interleave("S", 0, 2)
+        interleave("S", 0, 3)
+        interleave("S", 0, 4)
+        gather(2, late[:, 0:3, :].rearrange("p q c -> p (q c)"), 0, 768)
+        for q in range(3):
+            gather(3, late[:, 3 + q, :], q * QUARTER, (q + 1) * QUARTER)
+            interleave("S", 1, q)
+        quantize(0)
+        finish(0)
+        gather(2, late[:, 0, :], 768, 1024)
+        quantize(1)
+        finish(1)
+        gather(3, late[:, 1, :], 768, 1024)
+        quantize(2)
+        finish(2)
+        interleave("V", 1, 3)
+        interleave("V", 1, 4)
+        quantize(3)
+        quantize(4)
+        finish(3)
+        finish(4)

@@ -36,12 +36,12 @@ def tile_list_heads_gelu_kernel(tc, xT, w_words, w_scales, wgt, b, offs, out):
         weights = keep.tile([P, S], F32, name="weights")
         compact = keep.tile([P, QUARTER], F32, name="compact")
         identity = keep.tile([P, P], F32, name="identity")
-        spread = [[keep.tile([P, 2, GROUPS, 16], F32, name=f"spread{half}{h}") for h in range(2)] for half in range(2)]
+        spread = [keep.tile([P, 4, GROUPS, 16], F32, name=f"spread{h}") for h in range(2)]
         w_codes = keep.tile([P, M], U32, align_bytes=64, name="w_codes")
         w_planes = keep.tile([P, M], U8, align_bytes=64, name="w_planes")
         bias = keep.tile([P, M // P], F32, name="bias")
         early = keep.tile([P, 2, S], F32, name="early")
-        late = keep.tile([P, 6, QUARTER], F32, name="late")
+        late = keep.tile([P, 7, QUARTER], F32, name="late")
         grouped = [
             keep.tile([P, hi - lo, PACK], BF16, align_bytes=64, name=f"grouped{c}") for c, (lo, hi) in enumerate(CHUNKS)
         ]
@@ -67,18 +67,17 @@ def tile_list_heads_gelu_kernel(tc, xT, w_words, w_scales, wgt, b, offs, out):
 
         for h in range(2):
             nc.tensor.transpose(banks[6 + h][:, 0:P], compact[:, h * P : (h + 1) * P], identity[:])
-        for half in range(2):
+        for lo, hi in ((0, 1), (1, 4)):
             for h, copy in enumerate((nc.vector.tensor_copy, nc.scalar.copy)):
-                turned = banks[6 + h][:, 0:32].rearrange("p (g q) -> p q g", q=4)[:, 2 * half : 2 * half + 2, :]
-                copy(spread[half][h][:], turned.unsqueeze(3).to_broadcast([P, 2, GROUPS, 16]))
-        for q in range(4):
+                turned = banks[6 + h][:, 0:32].rearrange("p (g q) -> p q g", q=4)[:, lo:hi, :]
+                copy(spread[h][:, lo:hi], turned.unsqueeze(3).to_broadcast([P, hi - lo, GROUPS, 16]))
+        for q in (0, 1, 3, 2):
             for h in range(2):
                 nc.tensor.transpose(
-                    banks[q][:, h * P : (h + 1) * P],
-                    spread[q // 2][h][:, q % 2].rearrange("p g r -> p (g r)"),
-                    identity[:],
+                    banks[q][:, h * P : (h + 1) * P], spread[h][:, q].rearrange("p g r -> p (g r)"), identity[:]
                 )
-            nc.scalar.copy(weights[:, q * QUARTER : (q + 1) * QUARTER], banks[q][:, 0:QUARTER])
+            copy = nc.scalar.copy if q else nc.vector.tensor_copy
+            copy(weights[:, q * QUARTER : (q + 1) * QUARTER], banks[q][:, 0:QUARTER])
 
         nc.sync.dma_start(w_codes[:].bitcast(I32), w_words[0].rearrange("p n i -> p (n i)").bitcast(I32))
         for q in range(4):
@@ -96,7 +95,7 @@ def tile_list_heads_gelu_kernel(tc, xT, w_words, w_scales, wgt, b, offs, out):
             lo, hi = CHUNKS[c]
             q = lo // QUARTER
             if pair:
-                rows = slice(q, q + 4, 3) if q < 3 else slice(0, 2)
+                rows = slice(q, q + 4, 3) if q < 3 else slice(1, 7, 5)
                 src = late[:, rows, lo - q * QUARTER : hi - q * QUARTER]
             else:
                 src = early[:, :, lo:hi]
@@ -135,23 +134,24 @@ def tile_list_heads_gelu_kernel(tc, xT, w_words, w_scales, wgt, b, offs, out):
         gather(0, early[:, 0, 0:256], 0, 256)
         gather(0, early[:, 0, 256:512], 256, 512)
         gather(0, early[:, 0, 512:1024], 512, 1024)
-        gather(1, early[:, 1, 0:512], 0, 512)
+        gather(1, early[:, 1, 0:640], 0, 640)
         interleave("S", 0, 0)
         interleave("S", 0, 1)
-        gather(1, early[:, 1, 512:1024], 512, 1024)
+        gather(1, early[:, 1, 640:1024], 640, 1024)
         interleave("S", 0, 2)
         interleave("S", 0, 3)
         interleave("S", 0, 4)
         gather(2, late[:, 0:3, :].rearrange("p q c -> p (q c)"), 0, 768)
-        for q in range(3):
+        for q in range(2):
             gather(3, late[:, 3 + q, :], q * QUARTER, (q + 1) * QUARTER)
             interleave("S", 1, q)
+        gather(3, late[:, 5:7, :].rearrange("p q c -> p (q c)"), 512, 1024)
+        interleave("S", 1, 2)
         quantize(0)
         finish(0)
-        gather(2, late[:, 0, :], 768, 1024)
         quantize(1)
         finish(1)
-        gather(3, late[:, 1, :], 768, 1024)
+        gather(2, late[:, 1, :], 768, 1024)
         quantize(2)
         finish(2)
         interleave("V", 1, 3)

@@ -134,10 +134,10 @@ def tile_list_heads_gelu_kernel(tc, xT, w_words, w_scales, wgt, b, offs, out):
         gather(0, early[:, 0, 0:256], 0, 256)
         gather(0, early[:, 0, 256:512], 256, 512)
         gather(0, early[:, 0, 512:1024], 512, 1024)
-        gather(1, early[:, 1, 0:640], 0, 640)
+        gather(1, early[:, 1, 0:544], 0, 544)
         interleave("S", 0, 0)
         interleave("S", 0, 1)
-        gather(1, early[:, 1, 640:1024], 640, 1024)
+        gather(1, early[:, 1, 544:1024], 544, 1024)
         interleave("S", 0, 2)
         interleave("S", 0, 3)
         interleave("S", 0, 4)

@@ -41,7 +41,7 @@ def tile_list_heads_gelu_kernel(tc, xT, w_words, w_scales, wgt, b, offs, out):
         w_planes = keep.tile([P, M], U8, align_bytes=64, name="w_planes")
         bias = keep.tile([P, M // P], F32, name="bias")
         early = keep.tile([P, 2, S], F32, name="early")
-        late = keep.tile([P, 7, QUARTER], F32, name="late")
+        late = keep.tile([P, 6, QUARTER], F32, name="late")
         grouped = [
             keep.tile([P, hi - lo, PACK], BF16, align_bytes=64, name=f"grouped{c}") for c, (lo, hi) in enumerate(CHUNKS)
         ]
@@ -95,7 +95,7 @@ def tile_list_heads_gelu_kernel(tc, xT, w_words, w_scales, wgt, b, offs, out):
             lo, hi = CHUNKS[c]
             q = lo // QUARTER
             if pair:
-                rows = slice(q, q + 4, 3) if q < 3 else slice(1, 7, 5)
+                rows = slice(q, q + 4, 3) if q < 3 else slice(0, 2)
                 src = late[:, rows, lo - q * QUARTER : hi - q * QUARTER]
             else:
                 src = early[:, :, lo:hi]
@@ -142,16 +142,15 @@ def tile_list_heads_gelu_kernel(tc, xT, w_words, w_scales, wgt, b, offs, out):
         interleave("S", 0, 3)
         interleave("S", 0, 4)
         gather(2, late[:, 0:3, :].rearrange("p q c -> p (q c)"), 0, 768)
-        for q in range(2):
+        for q in range(3):
             gather(3, late[:, 3 + q, :], q * QUARTER, (q + 1) * QUARTER)
             interleave("S", 1, q)
-        gather(3, late[:, 5:7, :].rearrange("p q c -> p (q c)"), 512, 1024)
-        interleave("S", 1, 2)
         quantize(0)
         finish(0)
+        gather(2, late[:, 0, :], 768, 1024)
         quantize(1)
         finish(1)
-        gather(2, late[:, 1, :], 768, 1024)
+        gather(3, late[:, 1, :], 768, 1024)
         quantize(2)
         finish(2)
         interleave("V", 1, 3)

@@ -21,6 +21,7 @@ P = 128
 PACK = 4
 GROUPS = 8
 QUARTER = S // 4
+CUT = 800
 CHUNKS = ((0, 256), (256, 512), (512, 768), (768, 896), (896, 1024))
 
 
@@ -41,10 +42,16 @@ def tile_list_heads_gelu_kernel(tc, xT, w_words, w_scales, wgt, b, offs, out):
         w_planes = keep.tile([P, M], U8, align_bytes=64, name="w_planes")
         bias = keep.tile([P, M // P], F32, name="bias")
         early = keep.tile([P, 2, S], F32, name="early")
-        late = keep.tile([P, 6, QUARTER], F32, name="late")
-        grouped = [
-            keep.tile([P, hi - lo, PACK], BF16, align_bytes=64, name=f"grouped{c}") for c, (lo, hi) in enumerate(CHUNKS)
+        late = keep.tile([P, 2, CUT], F32, name="late")
+        spans = ((0, 256), (256, 512), (512, 896), (896, 1024))
+        tiles = [
+            keep.tile([P, hi - lo, PACK], BF16, align_bytes=64, name=f"grouped{c}") for c, (lo, hi) in enumerate(spans)
         ]
+
+        def grouped(lo, hi):
+            c = max(i for i, span in enumerate(spans) if span[0] <= lo)
+            return tiles[c][:, lo - spans[c][0] : hi - spans[c][0], :]
+
         codes = keep.tile([P, S], U32, align_bytes=64, name="codes")
         scales = keep.tile([P, S], U8, align_bytes=64, name="scales")
         warm = keep.tile([P, 2], F32, name="warm")
@@ -53,7 +60,8 @@ def tile_list_heads_gelu_kernel(tc, xT, w_words, w_scales, wgt, b, offs, out):
 
         runs = wgt.rearrange("p (q c) -> (p q) c", c=QUARTER)
         for half in range(2):
-            nc.sync.dma_start(compact[16 * half : 16 * half + 16, :], runs[256 * half : 256 * half + 256 : 17, :])
+            queue = nc.scalar if half else nc.sync
+            queue.dma_start(compact[16 * half : 16 * half + 16, :], runs[256 * half : 256 * half + 256 : 17, :])
         nc.sync.dma_start(table[0][:], planes[0])
         nc.sync.dma_start(offsets[:], offs)
         for i in range(1, PACK):
@@ -71,13 +79,15 @@ def tile_list_heads_gelu_kernel(tc, xT, w_words, w_scales, wgt, b, offs, out):
             for h, copy in enumerate((nc.vector.tensor_copy, nc.scalar.copy)):
                 turned = banks[6 + h][:, 0:32].rearrange("p (g q) -> p q g", q=4)[:, lo:hi, :]
                 copy(spread[h][:, lo:hi], turned.unsqueeze(3).to_broadcast([P, hi - lo, GROUPS, 16]))
-        for q in (0, 1, 3, 2):
-            for h in range(2):
+        for bank, (lo, hi) in enumerate(((0, 2), (2, 4), (6, 8), (4, 6))):
+            for j in range(lo, hi):
                 nc.tensor.transpose(
-                    banks[q][:, h * P : (h + 1) * P], spread[h][:, q].rearrange("p g r -> p (g r)"), identity[:]
+                    banks[bank][:, (j - lo) * P : (j - lo + 1) * P],
+                    spread[j % 2][:, j // 2].rearrange("p g r -> p (g r)"),
+                    identity[:],
                 )
-            copy = nc.scalar.copy if q else nc.vector.tensor_copy
-            copy(weights[:, q * QUARTER : (q + 1) * QUARTER], banks[q][:, 0:QUARTER])
+            copy = nc.scalar.copy if bank else nc.vector.tensor_copy
+            copy(weights[:, lo * P : hi * P], banks[bank][:, 0 : (hi - lo) * P])
 
         nc.sync.dma_start(w_codes[:].bitcast(I32), w_words[0].rearrange("p n i -> p (n i)").bitcast(I32))
         for q in range(4):
@@ -91,15 +101,16 @@ def tile_list_heads_gelu_kernel(tc, xT, w_words, w_scales, wgt, b, offs, out):
         def gather(i, dst, lo, hi):
             nc.vector.tensor_tensor(dst, table[i][:].indirect(offsets[:, lo // 16 : hi // 16]), weights[:, lo:hi], MULT)
 
-        def interleave(engine, pair, c):
-            lo, hi = CHUNKS[c]
-            q = lo // QUARTER
-            if pair:
-                rows = slice(q, q + 4, 3) if q < 3 else slice(0, 2)
-                src = late[:, rows, lo - q * QUARTER : hi - q * QUARTER]
-            else:
+        held = late[:, 0, 0:512].rearrange("p (t c) -> p t c", t=2)
+
+        def interleave(engine, pair, lo, hi):
+            if pair == 0:
                 src = early[:, :, lo:hi]
-            dst = grouped[c][:, :, 2 * pair : 2 * pair + 2]
+            elif lo < CUT:
+                src = late[:, :, lo:hi]
+            else:
+                src = held[:, :, lo - CUT : hi - CUT]
+            dst = grouped(lo, hi)[:, :, 2 * pair : 2 * pair + 2]
             if engine == "V":
                 nc.vector.tensor_copy(dst, src.rearrange("p t c -> p c t"))
             else:
@@ -110,7 +121,7 @@ def tile_list_heads_gelu_kernel(tc, xT, w_words, w_scales, wgt, b, offs, out):
             nc.vector.quantize_mx(
                 out=codes[:, lo:hi].bitcast(FP8X4),
                 scales=scales[:, lo:hi],
-                in_=grouped[c][:].rearrange("p c t -> p (c t)"),
+                in_=grouped(lo, hi).rearrange("p c t -> p (c t)"),
             )
             for m in range(M // P):
                 nc.tensor.matmul_mx(
@@ -129,32 +140,34 @@ def tile_list_heads_gelu_kernel(tc, xT, w_words, w_scales, wgt, b, offs, out):
                 nc.scalar.activation(
                     result[:, m, lo:hi], banks[(2 * c + m) % 8][:, 0 : hi - lo], GELU, bias=bias[:, m : m + 1]
                 )
-                nc.sync.dma_start(out[m * P : (m + 1) * P, lo:hi], result[:, m, lo:hi])
+                if not (c >= 3):
+                    nc.sync.dma_start(out[m * P : (m + 1) * P, lo:hi], result[:, m, lo:hi])
+            if c >= 3:
+                nc.sync.dma_start(out.rearrange("(m p) s -> p m s", p=P)[:, :, lo:hi], result[:, :, lo:hi])
 
         gather(0, early[:, 0, 0:256], 0, 256)
         gather(0, early[:, 0, 256:512], 256, 512)
         gather(0, early[:, 0, 512:1024], 512, 1024)
         gather(1, early[:, 1, 0:544], 0, 544)
-        interleave("S", 0, 0)
-        interleave("S", 0, 1)
+        interleave("S", 0, 0, 256)
+        interleave("S", 0, 256, 512)
         gather(1, early[:, 1, 544:1024], 544, 1024)
-        interleave("S", 0, 2)
-        interleave("S", 0, 3)
-        interleave("S", 0, 4)
-        gather(2, late[:, 0:3, :].rearrange("p q c -> p (q c)"), 0, 768)
-        for q in range(3):
-            gather(3, late[:, 3 + q, :], q * QUARTER, (q + 1) * QUARTER)
-            interleave("S", 1, q)
+        interleave("S", 0, 512, 896)
+        interleave("S", 0, 896, 1024)
+        gather(2, late[:, 0, :], 0, CUT)
+        for lo, hi in ((0, 256), (256, 512), (512, CUT)):
+            gather(3, late[:, 1, lo:hi], lo, hi)
+            interleave("S", 1, lo, hi)
         quantize(0)
         finish(0)
-        gather(2, late[:, 0, :], 768, 1024)
+        gather(2, held[:, 0, 0 : S - CUT], CUT, S)
         quantize(1)
         finish(1)
-        gather(3, late[:, 1, :], 768, 1024)
+        gather(3, held[:, 1, 0 : S - CUT], CUT, S)
         quantize(2)
         finish(2)
-        interleave("V", 1, 3)
-        interleave("V", 1, 4)
+        interleave("V", 1, CUT, 896)
+        interleave("V", 1, 896, S)
         quantize(3)
         quantize(4)
         finish(3)

@@ -21,7 +21,7 @@ P = 128
 PACK = 4
 GROUPS = 8
 QUARTER = S // 4
-CUT = 800
+CUT = 768
 CHUNKS = ((0, 256), (256, 512), (512, 768), (768, 896), (896, 1024))
 
 

@@ -79,7 +79,7 @@ def tile_list_heads_gelu_kernel(tc, xT, w_words, w_scales, wgt, b, offs, out):
             for h, copy in enumerate((nc.vector.tensor_copy, nc.scalar.copy)):
                 turned = banks[6 + h][:, 0:32].rearrange("p (g q) -> p q g", q=4)[:, lo:hi, :]
                 copy(spread[h][:, lo:hi], turned.unsqueeze(3).to_broadcast([P, hi - lo, GROUPS, 16]))
-        for bank, (lo, hi) in enumerate(((0, 2), (2, 4), (6, 8), (4, 6))):
+        for bank, (lo, hi) in enumerate(((0, 2), (6, 8), (4, 6), (2, 4))):
             for j in range(lo, hi):
                 nc.tensor.transpose(
                     banks[bank][:, (j - lo) * P : (j - lo + 1) * P],
@@ -146,16 +146,17 @@ def tile_list_heads_gelu_kernel(tc, xT, w_words, w_scales, wgt, b, offs, out):
                 nc.sync.dma_start(out.rearrange("(m p) s -> p m s", p=P)[:, :, lo:hi], result[:, :, lo:hi])
 
         gather(0, early[:, 0, 0:256], 0, 256)
-        gather(0, early[:, 0, 256:512], 256, 512)
-        gather(0, early[:, 0, 512:1024], 512, 1024)
-        gather(1, early[:, 1, 0:544], 0, 544)
+        gather(0, early[:, 0, 768:1024], 768, 1024)
+        gather(0, early[:, 0, 256:768], 256, 768)
+        gather(1, early[:, 1, 0:416], 0, 416)
         interleave("S", 0, 0, 256)
-        interleave("S", 0, 256, 512)
-        gather(1, early[:, 1, 544:1024], 544, 1024)
+        interleave("S", 0, 256, 416)
+        gather(1, early[:, 1, 416:1024], 416, 1024)
+        interleave("S", 0, 416, 512)
         interleave("S", 0, 512, 896)
         interleave("S", 0, 896, 1024)
         gather(2, late[:, 0, :], 0, CUT)
-        for lo, hi in ((0, 256), (256, 512), (512, CUT)):
+        for lo, hi in ((0, 128), (128, 256), (256, 512), (512, CUT)):
             gather(3, late[:, 1, lo:hi], lo, hi)
             interleave("S", 1, lo, hi)
         quantize(0)

@@ -140,10 +140,8 @@ def tile_list_heads_gelu_kernel(tc, xT, w_words, w_scales, wgt, b, offs, out):
                 nc.scalar.activation(
                     result[:, m, lo:hi], banks[(2 * c + m) % 8][:, 0 : hi - lo], GELU, bias=bias[:, m : m + 1]
                 )
-                if not (c >= 3):
-                    nc.sync.dma_start(out[m * P : (m + 1) * P, lo:hi], result[:, m, lo:hi])
-            if c >= 3:
-                nc.sync.dma_start(out.rearrange("(m p) s -> p m s", p=P)[:, :, lo:hi], result[:, :, lo:hi])
+                if hi % 256 == 0:
+                    nc.sync.dma_start(out[m * P : (m + 1) * P, hi - 256 : hi], result[:, m, hi - 256 : hi])
 
         gather(0, early[:, 0, 0:256], 0, 256)
         gather(0, early[:, 0, 768:1024], 768, 1024)

@@ -22,6 +22,7 @@ PACK = 4
 GROUPS = 8
 QUARTER = S // 4
 CUT = 768
+AHEAD = 832
 CHUNKS = ((0, 256), (256, 512), (512, 768), (768, 896), (896, 1024))
 
 
@@ -42,7 +43,7 @@ def tile_list_heads_gelu_kernel(tc, xT, w_words, w_scales, wgt, b, offs, out):
         w_planes = keep.tile([P, M], U8, align_bytes=64, name="w_planes")
         bias = keep.tile([P, M // P], F32, name="bias")
         early = keep.tile([P, 2, S], F32, name="early")
-        late = keep.tile([P, 2, CUT], F32, name="late")
+        late = keep.tile([P, 2 * AHEAD], F32, name="late")
         spans = ((0, 256), (256, 512), (512, 896), (896, 1024))
         tiles = [
             keep.tile([P, hi - lo, PACK], BF16, align_bytes=64, name=f"grouped{c}") for c, (lo, hi) in enumerate(spans)
@@ -75,18 +76,18 @@ def tile_list_heads_gelu_kernel(tc, xT, w_words, w_scales, wgt, b, offs, out):
 
         for h in range(2):
             nc.tensor.transpose(banks[6 + h][:, 0:P], compact[:, h * P : (h + 1) * P], identity[:])
-        for lo, hi in ((0, 1), (1, 4)):
+        for lo, hi in ((0, 1), (3, 4), (1, 3)):
             for h, copy in enumerate((nc.vector.tensor_copy, nc.scalar.copy)):
                 turned = banks[6 + h][:, 0:32].rearrange("p (g q) -> p q g", q=4)[:, lo:hi, :]
                 copy(spread[h][:, lo:hi], turned.unsqueeze(3).to_broadcast([P, hi - lo, GROUPS, 16]))
-        for bank, (lo, hi) in enumerate(((0, 2), (6, 8), (4, 6), (2, 4))):
+        for bank, (lo, hi) in enumerate(((0, 1), (1, 2), (6, 8), (4, 6), (2, 4))):
             for j in range(lo, hi):
                 nc.tensor.transpose(
                     banks[bank][:, (j - lo) * P : (j - lo + 1) * P],
                     spread[j % 2][:, j // 2].rearrange("p g r -> p (g r)"),
                     identity[:],
                 )
-            copy = nc.scalar.copy if bank else nc.vector.tensor_copy
+            copy = nc.scalar.copy if bank > 1 else nc.vector.tensor_copy
             copy(weights[:, lo * P : hi * P], banks[bank][:, 0 : (hi - lo) * P])
 
         nc.sync.dma_start(w_codes[:].bitcast(I32), w_words[0].rearrange("p n i -> p (n i)").bitcast(I32))
@@ -101,13 +102,14 @@ def tile_list_heads_gelu_kernel(tc, xT, w_words, w_scales, wgt, b, offs, out):
         def gather(i, dst, lo, hi):
             nc.vector.tensor_tensor(dst, table[i][:].indirect(offsets[:, lo // 16 : hi // 16]), weights[:, lo:hi], MULT)
 
-        held = late[:, 0, 0:512].rearrange("p (t c) -> p t c", t=2)
+        rows = late[:].rearrange("p (t c) -> p t c", t=2)
+        held = late[:, CUT : CUT + 2 * (AHEAD + 256 - CUT)].rearrange("p (t c) -> p t c", t=2)
 
         def interleave(engine, pair, lo, hi):
             if pair == 0:
                 src = early[:, :, lo:hi]
             elif lo < CUT:
-                src = late[:, :, lo:hi]
+                src = rows[:, :, lo:hi]
             else:
                 src = held[:, :, lo - CUT : hi - CUT]
             dst = grouped(lo, hi)[:, :, 2 * pair : 2 * pair + 2]
@@ -153,13 +155,13 @@ def tile_list_heads_gelu_kernel(tc, xT, w_words, w_scales, wgt, b, offs, out):
         interleave("S", 0, 416, 512)
         interleave("S", 0, 512, 896)
         interleave("S", 0, 896, 1024)
-        gather(2, late[:, 0, :], 0, CUT)
+        gather(2, rows[:, 0, :], 0, AHEAD)
         for lo, hi in ((0, 128), (128, 256), (256, 512), (512, CUT)):
-            gather(3, late[:, 1, lo:hi], lo, hi)
+            gather(3, rows[:, 1, lo:hi], lo, hi)
             interleave("S", 1, lo, hi)
         quantize(0)
         finish(0)
-        gather(2, held[:, 0, 0 : S - CUT], CUT, S)
+        gather(2, late[:, AHEAD:S], AHEAD, S)
         quantize(1)
         finish(1)
         gather(3, held[:, 1, 0 : S - CUT], CUT, S)

@@ -15,7 +15,6 @@ U8 = mybir.dt.uint8
 FP8X4 = mybir.dt.float8_e4m3fn_x4
 MULT = mybir.AluOpType.mult
 GELU = mybir.ActivationFunctionType.Gelu_apprx_tanh
-COPY = mybir.ActivationFunctionType.Copy
 
 P = 128
 PACK = 4
@@ -44,7 +43,7 @@ def tile_list_heads_gelu_kernel(tc, xT, w_words, w_scales, wgt, b, offs, out):
         bias = keep.tile([P, M // P], F32, name="bias")
         early = keep.tile([P, 2, S], F32, name="early")
         late = keep.tile([P, 2 * AHEAD], F32, name="late")
-        spans = ((0, 256), (256, 512), (512, 896), (896, 1024))
+        spans = ((0, 512), (512, 896), (896, 1024))
         tiles = [
             keep.tile([P, hi - lo, PACK], BF16, align_bytes=64, name=f"grouped{c}") for c, (lo, hi) in enumerate(spans)
         ]
@@ -116,7 +115,7 @@ def tile_list_heads_gelu_kernel(tc, xT, w_words, w_scales, wgt, b, offs, out):
             if engine == "V":
                 nc.vector.tensor_copy(dst, src.rearrange("p t c -> p c t"))
             else:
-                nc.scalar.activation(dst, src.rearrange("p t c -> p c t"), COPY)
+                nc.scalar.copy(dst, src.rearrange("p t c -> p c t"))
 
         def quantize(c):
             lo, hi = CHUNKS[c]
@@ -136,9 +135,9 @@ def tile_list_heads_gelu_kernel(tc, xT, w_words, w_scales, wgt, b, offs, out):
                     stop=True,
                 )
 
-        def finish(c):
+        def finish(c, halves=range(M // P)):
             lo, hi = CHUNKS[c]
-            for m in range(M // P):
+            for m in halves:
                 nc.scalar.activation(
                     result[:, m, lo:hi], banks[(2 * c + m) % 8][:, 0 : hi - lo], GELU, bias=bias[:, m : m + 1]
                 )
@@ -156,7 +155,7 @@ def tile_list_heads_gelu_kernel(tc, xT, w_words, w_scales, wgt, b, offs, out):
         interleave("S", 0, 512, 896)
         interleave("S", 0, 896, 1024)
         gather(2, rows[:, 0, :], 0, AHEAD)
-        for lo, hi in ((0, 128), (128, 256), (256, 512), (512, CUT)):
+        for lo, hi in ((0, 128), (128, 288), (288, 512), (512, CUT)):
             gather(3, rows[:, 1, lo:hi], lo, hi)
             interleave("S", 1, lo, hi)
         quantize(0)
@@ -171,5 +170,6 @@ def tile_list_heads_gelu_kernel(tc, xT, w_words, w_scales, wgt, b, offs, out):
         interleave("V", 1, 896, S)
         quantize(3)
         quantize(4)
-        finish(3)
-        finish(4)
+        for m in range(M // P):
+            finish(3, [m])
+            finish(4, [m])

@@ -21,8 +21,7 @@ PACK = 4
 GROUPS = 8
 QUARTER = S // 4
 CUT = 768
-AHEAD = 832
-CHUNKS = ((0, 256), (256, 512), (512, 768), (768, 896), (896, 1024))
+AHEAD = 768
 
 
 def tile_list_heads_gelu_kernel(tc, xT, w_words, w_scales, wgt, b, offs, out):
@@ -117,39 +116,43 @@ def tile_list_heads_gelu_kernel(tc, xT, w_words, w_scales, wgt, b, offs, out):
             else:
                 nc.scalar.copy(dst, src.rearrange("p t c -> p c t"))
 
-        def quantize(c):
-            lo, hi = CHUNKS[c]
+        def quantize(lo, hi):
             nc.vector.quantize_mx(
                 out=codes[:, lo:hi].bitcast(FP8X4),
                 scales=scales[:, lo:hi],
                 in_=grouped(lo, hi).rearrange("p c t -> p (c t)"),
             )
-            for m in range(M // P):
-                nc.tensor.matmul_mx(
-                    out=banks[(2 * c + m) % 8][:, 0 : hi - lo],
-                    lhsT=w_codes[:, m * P : (m + 1) * P].bitcast(FP8X4),
-                    lhsT_scale=w_planes[:, m * P : (m + 1) * P],
-                    rhs=codes[:, lo:hi].bitcast(FP8X4),
-                    rhs_scale=scales[:, lo:hi],
-                    start=True,
-                    stop=True,
-                )
 
-        def finish(c, halves=range(M // P)):
-            lo, hi = CHUNKS[c]
-            for m in halves:
-                nc.scalar.activation(
-                    result[:, m, lo:hi], banks[(2 * c + m) % 8][:, 0 : hi - lo], GELU, bias=bias[:, m : m + 1]
-                )
-                if hi % 256 == 0:
-                    nc.sync.dma_start(out[m * P : (m + 1) * P, hi - 256 : hi], result[:, m, hi - 256 : hi])
+        def multiply(m, lo, hi, sums):
+            nc.tensor.matmul_mx(
+                out=sums,
+                lhsT=w_codes[:, m * P : (m + 1) * P].bitcast(FP8X4),
+                lhsT_scale=w_planes[:, m * P : (m + 1) * P],
+                rhs=codes[:, lo:hi].bitcast(FP8X4),
+                rhs_scale=scales[:, lo:hi],
+                start=True,
+                stop=True,
+            )
+
+        def finish(m, lo, hi, sums):
+            nc.scalar.activation(result[:, m, lo:hi], sums, GELU, bias=bias[:, m : m + 1])
+
+        def store(m, lo, hi):
+            nc.sync.dma_start(out[m * P : (m + 1) * P, lo:hi], result[:, m, lo:hi])
+
+        def whole(lo, hi, pair):
+            quantize(lo, hi)
+            for m in range(M // P):
+                multiply(m, lo, hi, pair[m][:, 0 : hi - lo])
+            for m in range(M // P):
+                finish(m, lo, hi, pair[m][:, 0 : hi - lo])
+                store(m, lo, hi)
 
         gather(0, early[:, 0, 0:256], 0, 256)
         gather(0, early[:, 0, 768:1024], 768, 1024)
         gather(0, early[:, 0, 256:768], 256, 768)
         gather(1, early[:, 1, 0:416], 0, 416)
-        interleave("S", 0, 0, 256)
-        interleave("S", 0, 256, 416)
+        interleave("S", 0, 0, 416)
         gather(1, early[:, 1, 416:1024], 416, 1024)
         interleave("S", 0, 416, 512)
         interleave("S", 0, 512, 896)
@@ -158,18 +161,25 @@ def tile_list_heads_gelu_kernel(tc, xT, w_words, w_scales, wgt, b, offs, out):
         for lo, hi in ((0, 128), (128, 288), (288, 512), (512, CUT)):
             gather(3, rows[:, 1, lo:hi], lo, hi)
             interleave("S", 1, lo, hi)
-        quantize(0)
-        finish(0)
+        whole(0, 256, banks[0:2])
         gather(2, late[:, AHEAD:S], AHEAD, S)
-        quantize(1)
-        finish(1)
+        whole(256, 512, banks[2:4])
         gather(3, held[:, 1, 0 : S - CUT], CUT, S)
-        quantize(2)
-        finish(2)
+        for lo in (512, 640):
+            quantize(lo, lo + 128)
+            multiply(0, lo, lo + 128, banks[4][:, lo - 512 : lo - 384])
+        multiply(1, 512, CUT, banks[5][:, 0:256])
+        for m in range(M // P):
+            finish(m, 512, CUT, banks[4 + m][:, 0:256])
+            store(m, 512, CUT)
         interleave("V", 1, CUT, 896)
         interleave("V", 1, 896, S)
-        quantize(3)
-        quantize(4)
-        for m in range(M // P):
-            finish(3, [m])
-            finish(4, [m])
+        for lo, bank in ((CUT, banks[6]), (896, banks[0])):
+            quantize(lo, lo + 128)
+            multiply(0, lo, lo + 128, bank[:, 0:128])
+            multiply(1, lo, lo + 128, banks[7][:, lo - CUT : lo - CUT + 128])
+        finish(0, CUT, 896, banks[6][:, 0:128])
+        finish(0, 896, S, banks[0][:, 0:128])
+        store(0, CUT, S)
+        finish(1, CUT, S, banks[7][:, 0 : S - CUT])
+        store(1, CUT, S)

@@ -74,11 +74,12 @@ def tile_list_heads_gelu_kernel(tc, xT, w_words, w_scales, wgt, b, offs, out):
 
         for h in range(2):
             nc.tensor.transpose(banks[6 + h][:, 0:P], compact[:, h * P : (h + 1) * P], identity[:])
-        for lo, hi in ((0, 1), (3, 4), (1, 3)):
+        for steps in (((0, 1), (0, 1)), ((1, 2), (2, 4)), ((2, 4), (1, 2))):
             for h, copy in enumerate((nc.vector.tensor_copy, nc.scalar.copy)):
+                lo, hi = steps[h]
                 turned = banks[6 + h][:, 0:32].rearrange("p (g q) -> p q g", q=4)[:, lo:hi, :]
                 copy(spread[h][:, lo:hi], turned.unsqueeze(3).to_broadcast([P, hi - lo, GROUPS, 16]))
-        for bank, (lo, hi) in enumerate(((0, 1), (1, 2), (6, 8), (4, 6), (2, 4))):
+        for bank, (lo, hi) in enumerate(((0, 1), (1, 2), (2, 3), (4, 6), (6, 8), (3, 4))):
             for j in range(lo, hi):
                 nc.tensor.transpose(
                     banks[bank][:, (j - lo) * P : (j - lo + 1) * P],
@@ -148,9 +149,8 @@ def tile_list_heads_gelu_kernel(tc, xT, w_words, w_scales, wgt, b, offs, out):
                 finish(m, lo, hi, pair[m][:, 0 : hi - lo])
                 store(m, lo, hi)
 
-        gather(0, early[:, 0, 0:256], 0, 256)
-        gather(0, early[:, 0, 768:1024], 768, 1024)
-        gather(0, early[:, 0, 256:768], 256, 768)
+        gather(0, early[:, 0, 0:384], 0, 384)
+        gather(0, early[:, 0, 384:1024], 384, 1024)
         gather(1, early[:, 1, 0:416], 0, 416)
         interleave("S", 0, 0, 416)
         gather(1, early[:, 1, 416:1024], 416, 1024)

@@ -20,8 +20,8 @@ P = 128
 PACK = 4
 GROUPS = 8
 QUARTER = S // 4
-CUT = 768
-AHEAD = 768
+EIGHTH = S // 8
+SHARE = 768
 
 
 def tile_list_heads_gelu_kernel(tc, xT, w_words, w_scales, wgt, b, offs, out):
@@ -41,16 +41,8 @@ def tile_list_heads_gelu_kernel(tc, xT, w_words, w_scales, wgt, b, offs, out):
         w_planes = keep.tile([P, M], U8, align_bytes=64, name="w_planes")
         bias = keep.tile([P, M // P], F32, name="bias")
         early = keep.tile([P, 2, S], F32, name="early")
-        late = keep.tile([P, 2 * AHEAD], F32, name="late")
-        spans = ((0, 512), (512, 896), (896, 1024))
-        tiles = [
-            keep.tile([P, hi - lo, PACK], BF16, align_bytes=64, name=f"grouped{c}") for c, (lo, hi) in enumerate(spans)
-        ]
-
-        def grouped(lo, hi):
-            c = max(i for i, span in enumerate(spans) if span[0] <= lo)
-            return tiles[c][:, lo - spans[c][0] : hi - spans[c][0], :]
-
+        late = keep.tile([P, 2 * SHARE], F32, name="late")
+        grouped = keep.tile([P, S, PACK], BF16, align_bytes=64, name="grouped")
         codes = keep.tile([P, S], U32, align_bytes=64, name="codes")
         scales = keep.tile([P, S], U8, align_bytes=64, name="scales")
         warm = keep.tile([P, 2], F32, name="warm")
@@ -60,14 +52,13 @@ def tile_list_heads_gelu_kernel(tc, xT, w_words, w_scales, wgt, b, offs, out):
         runs = wgt.rearrange("p (q c) -> (p q) c", c=QUARTER)
         for half in range(2):
             queue = nc.scalar if half else nc.sync
-            queue.dma_start(compact[16 * half : 16 * half + 16, :], runs[256 * half : 256 * half + 256 : 17, :])
+            queue.dma_start(compact[96 + 16 * half : 112 + 16 * half, :], runs[256 * half : 256 * half + 256 : 17, :])
         nc.sync.dma_start(table[0][:], planes[0])
         nc.sync.dma_start(offsets[:], offs)
         for i in range(1, PACK):
             nc.sync.dma_start(table[i][:], planes[i])
         make_identity(nc, identity[:])
-        nc.vector.memset(compact[32:64, :], 0.0)
-        nc.vector.memset(compact[64:128, :], 0.0)
+        nc.vector.memset(compact[0:96, :], 0.0)
         nc.vector.memset(warm[:, 0:1], 0.0)
         nc.scalar.activation(warm[:, 1:2], warm[:, 0:1], GELU)
         nc.vector.memset(w_planes[:].bitcast(U32), 0)
@@ -77,7 +68,7 @@ def tile_list_heads_gelu_kernel(tc, xT, w_words, w_scales, wgt, b, offs, out):
         for steps in (((0, 1), (0, 1)), ((1, 2), (2, 4)), ((2, 4), (1, 2))):
             for h, copy in enumerate((nc.vector.tensor_copy, nc.scalar.copy)):
                 lo, hi = steps[h]
-                turned = banks[6 + h][:, 0:32].rearrange("p (g q) -> p q g", q=4)[:, lo:hi, :]
+                turned = banks[6 + h][:, 96:P].rearrange("p (g q) -> p q g", q=4)[:, lo:hi, :]
                 copy(spread[h][:, lo:hi], turned.unsqueeze(3).to_broadcast([P, hi - lo, GROUPS, 16]))
         for bank, (lo, hi) in enumerate(((0, 1), (1, 2), (2, 3), (4, 6), (6, 8), (3, 4))):
             for j in range(lo, hi):
@@ -101,27 +92,14 @@ def tile_list_heads_gelu_kernel(tc, xT, w_words, w_scales, wgt, b, offs, out):
         def gather(i, dst, lo, hi):
             nc.vector.tensor_tensor(dst, table[i][:].indirect(offsets[:, lo // 16 : hi // 16]), weights[:, lo:hi], MULT)
 
-        rows = late[:].rearrange("p (t c) -> p t c", t=2)
-        held = late[:, CUT : CUT + 2 * (AHEAD + 256 - CUT)].rearrange("p (t c) -> p t c", t=2)
-
-        def interleave(engine, pair, lo, hi):
-            if pair == 0:
-                src = early[:, :, lo:hi]
-            elif lo < CUT:
-                src = rows[:, :, lo:hi]
-            else:
-                src = held[:, :, lo - CUT : hi - CUT]
-            dst = grouped(lo, hi)[:, :, 2 * pair : 2 * pair + 2]
-            if engine == "V":
-                nc.vector.tensor_copy(dst, src.rearrange("p t c -> p c t"))
-            else:
-                nc.scalar.copy(dst, src.rearrange("p t c -> p c t"))
+        def interleave(copy, src, pair, lo, hi):
+            copy(grouped[:, lo:hi, 2 * pair : 2 * pair + 2], src.rearrange("p t c -> p c t"))
 
         def quantize(lo, hi):
             nc.vector.quantize_mx(
                 out=codes[:, lo:hi].bitcast(FP8X4),
                 scales=scales[:, lo:hi],
-                in_=grouped(lo, hi).rearrange("p c t -> p (c t)"),
+                in_=grouped[:, lo:hi, :].rearrange("p c t -> p (c t)"),
             )
 
         def multiply(m, lo, hi, sums):
@@ -141,45 +119,47 @@ def tile_list_heads_gelu_kernel(tc, xT, w_words, w_scales, wgt, b, offs, out):
         def store(m, lo, hi):
             nc.sync.dma_start(out[m * P : (m + 1) * P, lo:hi], result[:, m, lo:hi])
 
-        def whole(lo, hi, pair):
-            quantize(lo, hi)
-            for m in range(M // P):
-                multiply(m, lo, hi, pair[m][:, 0 : hi - lo])
-            for m in range(M // P):
-                finish(m, lo, hi, pair[m][:, 0 : hi - lo])
-                store(m, lo, hi)
+        rows = late[:].rearrange("p (t c) -> p t c", t=2)
+        held = late[:, SHARE : SHARE + 2 * QUARTER].rearrange("p (t c) -> p t c", t=2)
 
         gather(0, early[:, 0, 0:384], 0, 384)
-        gather(0, early[:, 0, 384:1024], 384, 1024)
-        gather(1, early[:, 1, 0:416], 0, 416)
-        interleave("S", 0, 0, 416)
-        gather(1, early[:, 1, 416:1024], 416, 1024)
-        interleave("S", 0, 416, 512)
-        interleave("S", 0, 512, 896)
-        interleave("S", 0, 896, 1024)
-        gather(2, rows[:, 0, :], 0, AHEAD)
-        for lo, hi in ((0, 128), (128, 288), (288, 512), (512, CUT)):
+        gather(0, early[:, 0, 384:S], 384, S)
+        for lo, hi in ((0, 416), (416, S)):
+            gather(1, early[:, 1, lo:hi], lo, hi)
+            interleave(nc.scalar.copy, early[:, :, lo:hi], 0, lo, hi)
+        gather(2, rows[:, 0, :], 0, SHARE)
+        for lo, hi in ((0, 128), (128, 288), (288, 512), (512, SHARE)):
             gather(3, rows[:, 1, lo:hi], lo, hi)
-            interleave("S", 1, lo, hi)
-        whole(0, 256, banks[0:2])
-        gather(2, late[:, AHEAD:S], AHEAD, S)
-        whole(256, 512, banks[2:4])
-        gather(3, held[:, 1, 0 : S - CUT], CUT, S)
+            interleave(nc.scalar.copy, rows[:, :, lo:hi], 1, lo, hi)
+        quantize(0, 256)
+        for m in range(2):
+            multiply(m, 0, 256, banks[m][:, 0:256])
+        for m in range(2):
+            finish(m, 0, 256, banks[m][:, 0:256])
+            store(m, 0, 256)
+        gather(2, held[:, 0, :], SHARE, S)
+        quantize(256, 512)
+        for m in range(2):
+            multiply(m, 256, 512, banks[2 + m][:, 0:256])
+        for m in range(2):
+            finish(m, 256, 512, banks[2 + m][:, 0:256])
+            store(m, 256, 512)
+        gather(3, held[:, 1, :], SHARE, S)
         for lo in (512, 640):
-            quantize(lo, lo + 128)
-            multiply(0, lo, lo + 128, banks[4][:, lo - 512 : lo - 384])
-        multiply(1, 512, CUT, banks[5][:, 0:256])
-        for m in range(M // P):
-            finish(m, 512, CUT, banks[4 + m][:, 0:256])
-            store(m, 512, CUT)
-        interleave("V", 1, CUT, 896)
-        interleave("V", 1, 896, S)
-        for lo, bank in ((CUT, banks[6]), (896, banks[0])):
-            quantize(lo, lo + 128)
-            multiply(0, lo, lo + 128, bank[:, 0:128])
-            multiply(1, lo, lo + 128, banks[7][:, lo - CUT : lo - CUT + 128])
-        finish(0, CUT, 896, banks[6][:, 0:128])
-        finish(0, 896, S, banks[0][:, 0:128])
-        store(0, CUT, S)
-        finish(1, CUT, S, banks[7][:, 0 : S - CUT])
-        store(1, CUT, S)
+            quantize(lo, lo + EIGHTH)
+            multiply(0, lo, lo + EIGHTH, banks[4][:, lo - 512 : lo - 512 + EIGHTH])
+        multiply(1, 512, SHARE, banks[5][:, 0:256])
+        for m in range(2):
+            finish(m, 512, SHARE, banks[4 + m][:, 0:256])
+            store(m, 512, SHARE)
+        for lo in (SHARE, 896):
+            interleave(nc.vector.tensor_copy, held[:, :, lo - SHARE : lo - SHARE + EIGHTH], 1, lo, lo + EIGHTH)
+        for lo, bank in ((SHARE, banks[6]), (896, banks[0])):
+            quantize(lo, lo + EIGHTH)
+            multiply(0, lo, lo + EIGHTH, bank[:, 0:EIGHTH])
+            multiply(1, lo, lo + EIGHTH, banks[7][:, lo - SHARE : lo - SHARE + EIGHTH])
+        finish(0, SHARE, 896, banks[6][:, 0:EIGHTH])
+        finish(0, 896, S, banks[0][:, 0:EIGHTH])
+        store(0, SHARE, S)
+        finish(1, SHARE, S, banks[7][:, 0:QUARTER])
+        store(1, SHARE, S)

from contextlib import ExitStack

import concourse.mybir as mybir
from concourse.masks import make_identity

K, M, T, S = 512, 256, 2048, 1024
FLOPS = 2 * K * M * S

F32 = mybir.dt.float32
BF16 = mybir.dt.bfloat16
I32 = mybir.dt.int32
U32 = mybir.dt.uint32
U16 = mybir.dt.uint16
U8 = mybir.dt.uint8
FP8X4 = mybir.dt.float8_e4m3fn_x4
MULT = mybir.AluOpType.mult
GELU = mybir.ActivationFunctionType.Gelu_apprx_tanh

P = 128
PACK = 4
GROUPS = 8
QUARTER = S // 4
EIGHTH = S // 8
SHARE = 768


def tile_list_heads_gelu_kernel(tc, xT, w_words, w_scales, wgt, b, offs, out):
    nc = tc.nc
    planes = xT.rearrange("(p i) t -> i p t", i=PACK)
    with ExitStack() as ctx:
        keep = ctx.enter_context(tc.tile_pool(name="keep", bufs=1))
        psum = ctx.enter_context(tc.psum_pool(name="psum", bufs=1))

        offsets = keep.tile([P, S // 16], U16, name="offsets")
        table = [keep.tile([P, T], F32, name=f"table{i}") for i in range(PACK)]
        weights = keep.tile([P, S], F32, name="weights")
        compact = keep.tile([P, QUARTER], F32, name="compact")
        identity = keep.tile([P, P], F32, name="identity")
        spread = [keep.tile([P, 4, GROUPS, 16], F32, name=f"spread{h}") for h in range(2)]
        w_codes = keep.tile([P, M], U32, align_bytes=64, name="w_codes")
        w_planes = keep.tile([P, M], U8, align_bytes=64, name="w_planes")
        bias = keep.tile([P, M // P], F32, name="bias")
        early = keep.tile([P, 2, S], F32, name="early")
        late = keep.tile([P, 2 * SHARE], F32, name="late")
        grouped = keep.tile([P, S, PACK], BF16, align_bytes=64, name="grouped")
        codes = keep.tile([P, S], U32, align_bytes=64, name="codes")
        scales = keep.tile([P, S], U8, align_bytes=64, name="scales")
        warm = keep.tile([P, 2], F32, name="warm")
        result = keep.tile([P, M // P, S], F32, name="result")
        banks = [psum.tile([P, 512], F32, name=f"bank{i}") for i in range(8)]

        runs = wgt.rearrange("p (q c) -> (p q) c", c=QUARTER)
        for half in range(2):
            queue = nc.scalar if half else nc.sync
            queue.dma_start(compact[96 + 16 * half : 112 + 16 * half, :], runs[256 * half : 256 * half + 256 : 17, :])
        nc.sync.dma_start(table[0][:], planes[0])
        nc.sync.dma_start(offsets[:], offs)
        for i in range(1, PACK):
            nc.sync.dma_start(table[i][:], planes[i])
        make_identity(nc, identity[:])
        nc.vector.memset(compact[0:96, :], 0.0)
        nc.vector.memset(warm[:, 0:1], 0.0)
        nc.scalar.activation(warm[:, 1:2], warm[:, 0:1], GELU)
        nc.vector.memset(w_planes[:].bitcast(U32), 0)

        for h in range(2):
            nc.tensor.transpose(banks[6 + h][:, 0:P], compact[:, h * P : (h + 1) * P], identity[:])
        for steps in (((0, 1), (0, 1)), ((1, 2), (2, 4)), ((2, 4), (1, 2))):
            for h, copy in enumerate((nc.vector.tensor_copy, nc.scalar.copy)):
                lo, hi = steps[h]
                turned = banks[6 + h][:, 96:P].rearrange("p (g q) -> p q g", q=4)[:, lo:hi, :]
                copy(spread[h][:, lo:hi], turned.unsqueeze(3).to_broadcast([P, hi - lo, GROUPS, 16]))
        for bank, (lo, hi) in enumerate(((0, 1), (1, 2), (2, 3), (4, 6), (6, 8), (3, 4))):
            for j in range(lo, hi):
                nc.tensor.transpose(
                    banks[bank][:, (j - lo) * P : (j - lo + 1) * P],
                    spread[j % 2][:, j // 2].rearrange("p g r -> p (g r)"),
                    identity[:],
                )
            copy = nc.scalar.copy if bank > 1 else nc.vector.tensor_copy
            copy(weights[:, lo * P : hi * P], banks[bank][:, 0 : (hi - lo) * P])

        nc.sync.dma_start(w_codes[:].bitcast(I32), w_words[0].rearrange("p n i -> p (n i)").bitcast(I32))
        for q in range(4):
            nc.sync.dma_start(
                w_planes[32 * q : 32 * q + 4, :].bitcast(I32),
                w_scales[0, 4 * q : 4 * q + 4, :].bitcast(I32),
            )
        with nc.allow_non_contiguous_dma(reason="256 bias values, one a partition"):
            nc.sync.dma_start(bias[:], b.rearrange("(m p) -> p m", p=P))

        def gather(i, dst, lo, hi):
            nc.vector.tensor_tensor(dst, table[i][:].indirect(offsets[:, lo // 16 : hi // 16]), weights[:, lo:hi], MULT)

        def interleave(copy, src, pair, lo, hi):
            copy(grouped[:, lo:hi, 2 * pair : 2 * pair + 2], src.rearrange("p t c -> p c t"))

        def quantize(lo, hi):
            nc.vector.quantize_mx(
                out=codes[:, lo:hi].bitcast(FP8X4),
                scales=scales[:, lo:hi],
                in_=grouped[:, lo:hi, :].rearrange("p c t -> p (c t)"),
            )

        def multiply(m, lo, hi, sums):
            nc.tensor.matmul_mx(
                out=sums,
                lhsT=w_codes[:, m * P : (m + 1) * P].bitcast(FP8X4),
                lhsT_scale=w_planes[:, m * P : (m + 1) * P],
                rhs=codes[:, lo:hi].bitcast(FP8X4),
                rhs_scale=scales[:, lo:hi],
                start=True,
                stop=True,
            )

        def finish(m, lo, hi, sums):
            nc.scalar.activation(result[:, m, lo:hi], sums, GELU, bias=bias[:, m : m + 1])

        def store(m, lo, hi):
            nc.sync.dma_start(out[m * P : (m + 1) * P, lo:hi], result[:, m, lo:hi])

        rows = late[:].rearrange("p (t c) -> p t c", t=2)
        held = late[:, SHARE : SHARE + 2 * QUARTER].rearrange("p (t c) -> p t c", t=2)

        gather(0, early[:, 0, 0:384], 0, 384)
        gather(0, early[:, 0, 384:S], 384, S)
        for lo, hi in ((0, 416), (416, S)):
            gather(1, early[:, 1, lo:hi], lo, hi)
            interleave(nc.scalar.copy, early[:, :, lo:hi], 0, lo, hi)
        gather(2, rows[:, 0, :], 0, SHARE)
        for lo, hi in ((0, 128), (128, 288), (288, 512), (512, SHARE)):
            gather(3, rows[:, 1, lo:hi], lo, hi)
            interleave(nc.scalar.copy, rows[:, :, lo:hi], 1, lo, hi)
        quantize(0, 256)
        for m in range(2):
            multiply(m, 0, 256, banks[m][:, 0:256])
        for m in range(2):
            finish(m, 0, 256, banks[m][:, 0:256])
            store(m, 0, 256)
        gather(2, held[:, 0, :], SHARE, S)
        quantize(256, 512)
        for m in range(2):
            multiply(m, 256, 512, banks[2 + m][:, 0:256])
        for m in range(2):
            finish(m, 256, 512, banks[2 + m][:, 0:256])
            store(m, 256, 512)
        gather(3, held[:, 1, :], SHARE, S)
        for lo in (512, 640):
            quantize(lo, lo + EIGHTH)
            multiply(0, lo, lo + EIGHTH, banks[4][:, lo - 512 : lo - 512 + EIGHTH])
        multiply(1, 512, SHARE, banks[5][:, 0:256])
        for m in range(2):
            finish(m, 512, SHARE, banks[4 + m][:, 0:256])
            store(m, 512, SHARE)
        for lo in (SHARE, 896):
            interleave(nc.vector.tensor_copy, held[:, :, lo - SHARE : lo - SHARE + EIGHTH], 1, lo, lo + EIGHTH)
        for lo, bank in ((SHARE, banks[6]), (896, banks[0])):
            quantize(lo, lo + EIGHTH)
            multiply(0, lo, lo + EIGHTH, bank[:, 0:EIGHTH])
            multiply(1, lo, lo + EIGHTH, banks[7][:, lo - SHARE : lo - SHARE + EIGHTH])
        finish(0, SHARE, 896, banks[6][:, 0:EIGHTH])
        finish(0, 896, S, banks[0][:, 0:EIGHTH])
        store(0, SHARE, S)
        finish(1, SHARE, S, banks[7][:, 0:QUARTER])
        store(1, SHARE, S)
